import numpy as np
import ml_dtypes


def mxq(x, axis, fmt="e4m3"):
    dtype, down = {"e4m3": (ml_dtypes.float8_e4m3fn, 7), "e5m2": (ml_dtypes.float8_e5m2, 14)}[fmt]
    v = np.moveaxis(np.asarray(x, np.float32).astype(ml_dtypes.bfloat16).astype(np.float64), axis, -1)
    blocks = v.reshape(v.shape[:-1] + (-1, 32))
    amax = np.abs(blocks).max(-1, keepdims=True)
    byte = np.maximum(np.where(amax > 0, np.frexp(amax)[1] - 1 + 127, 0) - down, 1)
    scale = np.exp2(byte - 127.0)
    codes = (blocks / scale).astype(np.float32).astype(dtype).astype(np.float64)
    return np.moveaxis((codes * scale).reshape(v.shape), -1, axis)


WIDE = False


def mx_kscale(k):
    if not WIDE:
        return np.ones(k)
    levels = np.array([10, -10, 5, -5, 0])
    if k % 512:
        return np.exp2(np.random.permutation(np.resize(levels, k // 32))).repeat(32)
    a = np.empty((k // 512, 16))
    for p in range(k // 512):
        a[p, :8] = np.random.permutation(np.resize(levels, 8))
        for g in range(8):
            far = levels[np.abs(levels - a[p, g]) >= 10]
            a[p, g + 8] = far[np.random.randint(len(far))]
    return np.exp2(a.ravel()).repeat(32)


def f64(x):
    return np.asarray(x).astype(np.float64)


def striped(idx):
    return np.tile(idx.reshape(-1, 16).T, (8, 1)).astype(np.uint16)


def unstriped(offs):
    return offs[:16].T.reshape(-1).astype(np.int64)


E2M1 = np.array([0.0, 0.5, 1.0, 1.5, 2.0, 3.0, 4.0, 6.0, -0.0, -0.5, -1.0, -1.5, -2.0, -3.0, -4.0, -6.0])


def pack_weight(w, fmt):
    k, n = w.shape
    w = f64(np.asarray(w, np.float32).astype(ml_dtypes.bfloat16)).reshape(k // 32, 32, n)
    amax = np.abs(w).max(1)
    if fmt == "e4m3":
        byte = np.frexp(amax)[1] - 1 + 127 - 7
    else:
        mant, ex = np.frexp(amax / 6.0)
        byte = np.where(mant > 0.5, ex, ex - 1) + 127
    byte = np.clip(np.where(amax > 0, byte, 1), 1, 254)
    scaled = (w * np.exp2(127.0 - byte)[:, None, :]).reshape(k, n).astype(np.float32)
    by_word = np.ascontiguousarray(scaled.reshape(k // 512, 128, 4, n).transpose(0, 1, 3, 2))
    if fmt == "e4m3":
        words = by_word.astype(ml_dtypes.float8_e4m3fn).view(np.uint8)
    else:
        c = by_word.astype(ml_dtypes.float4_e2m1fn).view(np.uint8) & 0xF
        words = (c[..., 0::2] | (c[..., 1::2] << 4)).reshape(k // 512, 128, 2 * n)
    return np.ascontiguousarray(words), np.ascontiguousarray(byte.astype(np.uint8).reshape(k // 512, 16, n))


def unpack_weight(words, scales, fmt):
    g, _, n = scales.shape
    words = np.ascontiguousarray(words).reshape(g, 128, n, -1)
    if fmt == "e4m3":
        vals = words.view(ml_dtypes.float8_e4m3fn).astype(np.float64)
    else:
        nib = np.empty((g, 128, n, 4), np.uint8)
        nib[..., 0::2] = words & 0xF
        nib[..., 1::2] = words >> 4
        vals = E2M1[nib]
    vals = vals * np.repeat(np.exp2(scales.astype(np.float64) - 127.0), 8, axis=1)[..., None]
    return vals.transpose(0, 1, 3, 2).reshape(g * 512, n)


def relu(v):
    return np.maximum(v, 0.0)


K, T, E, C, H, TOP, COPIES = 512, 768, 8, 256, 512, 4, 576
PAD = 64


def by_expert(wq, xq):
    return np.concatenate([wq[e].T @ xq[:, e * C:(e + 1) * C] for e in range(E)], axis=1)


def setup_inputs():
    n = np.random.standard_normal
    s = mx_kscale(K)
    u = mx_kscale(H)
    left = TOP * T - E * C - COPIES
    deal = np.repeat(np.arange(E + 2), [C] * E + [COPIES, left]).reshape(TOP, T)[:, np.random.permutation(T)]
    deal = np.take_along_axis(deal, np.argsort(np.random.rand(TOP, T), axis=0), axis=0)
    for _ in range(8):
        s_, t_ = np.random.permutation(T).reshape(2, -1); r = np.random.randint(TOP, size=T // 2); x, y = deal[r, s_].copy(), deal[r, t_].copy()
        ok = ~((deal[:, s_] == y).any(0) | (deal[:, t_] == x).any(0)); deal[r[ok], s_[ok]] = y[ok]; deal[r[ok], t_[ok]] = x[ok]
    order = np.lexsort((np.random.rand(TOP * T), deal.reshape(-1)))[:E * C]
    slot_token = order % T
    pos = np.where(deal == E, E * C + np.arange(T), E * C + T + np.arange(T) % PAD).reshape(-1); pos[order] = np.arange(E * C); pos = pos.reshape(TOP, T)
    g = np.random.uniform(0.5, 1.5, (TOP, T)); g = g / g.sum(0)
    xf = n((K, T))
    x = pack_weight(xf * s[:, None], "e4m3")
    w1 = [pack_weight(m, "e2m1") for m in n((E, K, H)) / np.sqrt(K) / s[None, :, None] * u]
    w2 = [pack_weight(m, "e2m1") for m in n((E, H, K)) / np.sqrt(H) / u[None, :, None]]
    return {
        "x_words": x[0],
        "x_scales": x[1],
        "xr": (xf).astype(np.float32),
        "w1_words": np.stack([m[0] for m in w1]),
        "w1_scales": np.stack([m[1] for m in w1]),
        "w2_words": np.stack([m[0] for m in w2]),
        "w2_scales": np.stack([m[1] for m in w2]),
        "gate": np.stack([np.tile(r, (128, 1)) for r in g]).astype(np.float32),
        "offs": striped(slot_token),
        "pos1": striped(pos[0]),
        "pos2": striped(pos[1]),
        "pos3": striped(pos[2]),
        "pos4": striped(pos[3]),
    }


def reference(x_words, x_scales, xr, w1_words, w1_scales, w2_words, w2_scales, gate, offs, pos1, pos2, pos3, pos4):
    w1 = np.stack([unpack_weight(w1_words[e], w1_scales[e], "e2m1") for e in range(E)])
    w2 = np.stack([unpack_weight(w2_words[e], w2_scales[e], "e2m1") for e in range(E)])
    idx = unstriped(offs)
    xq = unpack_weight(x_words, x_scales, "e4m3")[:, idx]
    h = relu(by_expert(w1, xq))
    y = by_expert(w2, mxq(h, 0, "e4m3"))
    y = np.concatenate([y, f64(xr), np.zeros((K, PAD))], axis=1)
    out = sum(f64(gate[r, :1]) * y[:, unstriped(p)] for r, p in enumerate((pos1, pos2, pos3, pos4)))
    return out

@@ -1,0 +1,200 @@
+from contextlib import ExitStack
+
+import concourse.mybir as mybir
+from concourse.masks import make_identity
+
+K, T, E, C, H, TOP = 512, 768, 8, 256, 512, 4
+SLOTS = E * C
+PAD = 64
+COLS = SLOTS + T + PAD
+FLOPS = 2 * SLOTS * (K * H + H * K)
+
+F32 = mybir.dt.float32
+BF16 = mybir.dt.bfloat16
+I32 = mybir.dt.int32
+U32 = mybir.dt.uint32
+U16 = mybir.dt.uint16
+U8 = mybir.dt.uint8
+FP8X4 = mybir.dt.float8_e4m3fn_x4
+FP4X4 = mybir.dt.float4_e2m1fn_x4
+RELU = mybir.ActivationFunctionType.Relu
+MULT = mybir.AluOpType.mult
+ADD = mybir.AluOpType.add
+
+P = 128
+BANK = 512
+ROW_BLOCKS = K // P
+HALF = T // 2
+GATHER_CUTS = [0, 256, 512, 768, 1024, 1536, 2048]
+LAST_TILE = SLOTS // P - 1
+
+
+def tile_moe_cpy_mlp_relu_kernel(
+    tc, x_words, x_scales, xr, w1_words, w1_scales, w2_words, w2_scales, gate, offs, pos1, pos2, pos3, pos4, out
+):
+    nc = tc.nc
+    with ExitStack() as ctx:
+        keep = ctx.enter_context(tc.tile_pool(name="keep", bufs=1))
+        ring = ctx.enter_context(tc.tile_pool(name="ring", bufs=3))
+        psum = ctx.enter_context(tc.psum_pool(name="psum", bufs=1))
+
+        slot_list = keep.tile([P, SLOTS // 16], U16, name="slot_list")
+        pos_lists = [keep.tile([P, T // 16], U16, name="pos_list%d" % r) for r in range(TOP)]
+        xw = keep.tile([P, T], U32, name="xw", align_bytes=64)
+        xs = keep.tile([P, T], U8, name="xs", align_bytes=64)
+        w1w = keep.tile([P, E, 2 * H], U8, name="w1w", align_bytes=64)
+        w2w = keep.tile([P, E, 2 * K], U8, name="w2w", align_bytes=64)
+        w1s = keep.tile([P, E, H], U8, name="w1s", align_bytes=64)
+        w2s = keep.tile([P, E, K], U8, name="w2s", align_bytes=64)
+        gates = keep.tile([P, TOP, T], F32, name="gates")
+        ys = [keep.tile([P, COLS], F32, name="y%d" % b, align_bytes=64) for b in range(ROW_BLOCKS)]
+        ident = keep.tile([P, P], F32, name="ident", align_bytes=64)
+        hq = keep.tile([P, SLOTS], U32, name="hq", align_bytes=64)
+        hs = keep.tile([P, SLOTS], U8, name="hs", align_bytes=64)
+
+        wide = [psum.tile([P, BANK], F32, name="wide%d" % i) for i in range(4)]
+        turn = [psum.tile([P, BANK], F32, name="turn%d" % i) for i in range(2)]
+        back = [psum.tile([P, BANK], F32, name="back%d" % i) for i in range(2)]
+
+        nc.vector.memset(w1s[:].bitcast(I32), 0)
+        nc.vector.memset(ys[0][:, SLOTS + T :], 0.0)
+        nc.vector.memset(w2s[:].bitcast(I32), 0)
+        for b in range(1, ROW_BLOCKS):
+            nc.scalar.activation(ys[b][:, SLOTS + T :], ys[0][:, SLOTS + T :], RELU)
+        make_identity(nc, ident[:])
+
+        def load_scale_rows(plane, scales, q):
+            nc.sync.dma_start(
+                plane[32 * q : 32 * q + 4, :, :].bitcast(I32),
+                scales[:, 0, 4 * q : 4 * q + 4, :].rearrange("e r n -> r e n").bitcast(I32),
+            )
+
+        def load_words(tile, words, experts, cols):
+            nc.sync.dma_start(
+                tile[:, experts, cols].bitcast(I32),
+                words[experts, 0, :, cols].rearrange("e p n -> p e n").bitcast(I32),
+            )
+
+        everything = slice(0, 2 * H)
+        nc.sync.dma_start(slot_list[:], offs)
+        nc.sync.dma_start(xw[:].bitcast(I32), x_words[0].rearrange("p t d -> p (t d)").bitcast(I32))
+        for q in range(4):
+            rows = x_scales[0, 4 * q : 4 * q + 4, :].bitcast(I32)
+            nc.sync.dma_start(xs[32 * q : 32 * (q + 1), :].bitcast(I32), rows.unsqueeze(0).to_broadcast([8, 4, T // 4]))
+        load_words(w1w, w1_words, slice(0, 1), everything)
+        load_words(w1w, w1_words, slice(1, 2), everything)
+        for q in range(4):
+            load_scale_rows(w1s, w1_scales, q)
+        load_words(w1w, w1_words, slice(2, 4), everything)
+        for q in range(4):
+            load_scale_rows(w2s, w2_scales, q)
+        load_words(w2w, w2_words, slice(0, E), slice(0, 2 * P))
+        load_words(w1w, w1_words, slice(4, E), everything)
+        nc.sync.dma_start(ys[0][:, SLOTS : SLOTS + T], xr[0:P, :])
+        for r, pos in enumerate((pos1, pos2, pos3, pos4)):
+            nc.sync.dma_start(pos_lists[r][:], pos)
+            nc.sync.dma_start(gates[:, r, :], gate[r])
+        load_words(w2w, w2_words, slice(0, E), slice(2 * P, 2 * K))
+        for b in range(1, ROW_BLOCKS):
+            nc.sync.dma_start(ys[b][:, SLOTS : SLOTS + T], xr[b * P : (b + 1) * P, :])
+
+        gathered = {}
+
+        def gather_tokens(lo, hi):
+            words = keep.tile([P, hi - lo], U32, name="xg%d" % lo, align_bytes=64)
+            scale = keep.tile([P, hi - lo], U8, name="sg%d" % lo, align_bytes=64)
+            cut = slot_list[:, lo // 16 : hi // 16]
+            nc.vector.tensor_copy(words[:], xw[:].indirect(cut))
+            nc.vector.tensor_copy(scale[:], xs[:].indirect(cut))
+            for s in range(lo, hi, P):
+                gathered[s // P] = (words[:, s - lo : s - lo + P], scale[:, s - lo : s - lo + P])
+
+        def first_layer(g):
+            words, scale = gathered[g]
+            e = g * P // C
+            acc = wide[g % 4]
+            nc.tensor.matmul_mx(
+                out=acc[:], lhsT=words.bitcast(FP8X4), lhsT_scale=scale,
+                rhs=w1w[:, e, :].bitcast(FP4X4), rhs_scale=w1s[:, e, :], start=True, stop=True,
+            )
+            hb = ring.tile([P, H], BF16, name="hb", align_bytes=64, bufs=4)
+            dst = hb[:].rearrange("p (u m d) -> p u m d", u=2, d=2)
+            src = acc[:].rearrange("p (m u d) -> p u m d", u=2, d=2)
+            if g == LAST_TILE:
+                nc.vector.tensor_scalar_max(dst, src, 0.0)
+            else:
+                nc.scalar.activation(dst, src, RELU)
+            return hb
+
+        def turn_and_quantise(e, pair):
+            ht = ring.tile([P, 4 * C], BF16, name="ht", align_bytes=64)
+            split = e == E - 1
+            for s, hb in enumerate(pair):
+                bank = wide[0] if split and s == 0 else turn[e % 2]
+                words = hb[:].bitcast(F32)
+                for u in range(2):
+                    col = (2 * s + u) * P
+                    nc.tensor.transpose(bank[:, col : col + P], words[:, u * P : (u + 1) * P], ident[:])
+            dst = ht[:].bitcast(F32).rearrange("p (s c u) -> p s c u", s=2, u=2)
+            src = turn[e % 2][:].rearrange("p (s u c) -> p s c u", s=2, u=2)
+            if split:
+                nc.scalar.copy(dst[:, 0], wide[0][:].rearrange("p (s u c) -> p s c u", s=2, u=2)[:, 0])
+                nc.vector.tensor_copy(dst[:, 1], src[:, 1])
+            else:
+                nc.scalar.copy(dst, src)
+            cols = slice(e * C, (e + 1) * C)
+            nc.vector.quantize_mx(out=hq[:, cols].bitcast(FP8X4), scales=hs[:, cols], in_=ht[:])
+
+        def second_layer(b, experts, bank, copy):
+            for j, e in enumerate(experts):
+                cols = slice(e * C, (e + 1) * C)
+                nc.tensor.matmul_mx(
+                    out=bank[:, j * C : (j + 1) * C],
+                    lhsT=w2w[:, e, 2 * P * b : 2 * P * (b + 1)].bitcast(FP4X4), lhsT_scale=w2s[:, e, P * b : P * (b + 1)],
+                    rhs=hq[:, cols].bitcast(FP8X4), rhs_scale=hs[:, cols], start=True, stop=True,
+                )
+            copy(ys[b][:, experts[0] * C : (experts[-1] + 1) * C], bank[:, : len(experts) * C])
+
+        for e in range(E):
+            if e * C in GATHER_CUTS:
+                gather_tokens(e * C, GATHER_CUTS[GATHER_CUTS.index(e * C) + 1])
+            pair = [first_layer(2 * e), first_layer(2 * e + 1)]
+            if e == E - 2:
+                second_layer(0, [0, 1], back[0], nc.vector.tensor_copy)
+                second_layer(0, [2, 3], back[1], nc.vector.tensor_copy)
+                second_layer(0, [4, 5], back[0], nc.vector.tensor_copy)
+            turn_and_quantise(e, pair)
+            if e >= E - 2:
+                second_layer(0, [e], back[(e + 1) % 2], nc.vector.tensor_copy)
+
+        for b in range(ROW_BLOCKS):
+            last = b == ROW_BLOCKS - 1
+            if not last:
+                for pair in range(E // 2):
+                    second_layer(b + 1, [2 * pair, 2 * pair + 1], wide[(pair + 1) % 4], nc.scalar.copy)
+            products = []
+            for r in range(TOP):
+                prod = ring.tile([P, T], F32, name="prod", align_bytes=64, bufs=2 * TOP)
+                nc.vector.tensor_tensor(prod[:], ys[b][:].indirect(pos_lists[r][:]), gates[:, r, :], MULT)
+                products.append(prod)
+            summed = products[:-1] if last else products
+            for half in range(2):
+                total = turn[half]
+                for j in range(HALF // P):
+                    tok = half * HALF + j * P
+                    for r, prod in enumerate(summed):
+                        nc.tensor.matmul(
+                            total[:, j * P : (j + 1) * P], lhsT=prod[:, tok : tok + P], rhs=ident[:],
+                            start=(r == 0), stop=(r == len(summed) - 1), is_transpose=True,
+                        )
+                total_sb = ring.tile([P, HALF], F32, name="total_sb", align_bytes=64)
+                nc.scalar.copy(total_sb[:], total[:, :HALF])
+                for j in range(HALF // P):
+                    nc.tensor.transpose(back[half][:, j * P : (j + 1) * P], total_sb[:, j * P : (j + 1) * P], ident[:])
+                result = ring.tile([P, HALF], F32, name="result", align_bytes=64)
+                toks = slice(half * HALF, (half + 1) * HALF)
+                if last:
+                    nc.vector.tensor_tensor(result[:], back[half][:, :HALF], products[-1][:, toks], ADD)
+                else:
+                    nc.scalar.copy(result[:], back[half][:, :HALF])
+                nc.sync.dma_start(out[b * P : (b + 1) * P, toks], result[:])

@@ -26,7 +26,8 @@ BANK = 512
 ROW_BLOCKS = K // P
 HALF = T // 2
 GATHER_CUTS = [0, 256, 512, 768, 1024, 1536, 2048]
-LAST_TILE = SLOTS // P - 1
+EARLY = 2
+H_ON_VECTOR = {13, 15}
 
 
 def tile_moe_cpy_mlp_relu_kernel(
@@ -56,17 +57,18 @@ def tile_moe_cpy_mlp_relu_kernel(
         turn = [psum.tile([P, BANK], F32, name="turn%d" % i) for i in range(2)]
         back = [psum.tile([P, BANK], F32, name="back%d" % i) for i in range(2)]
 
-        nc.vector.memset(w1s[:].bitcast(I32), 0)
+        nc.vector.memset(w1s[:, :EARLY, :].bitcast(I32), 0)
+        nc.vector.memset(w1s[:, EARLY:, :].bitcast(I32), 0)
+        nc.gpsimd.memset(w2s[:].bitcast(I32), 0)
         nc.vector.memset(ys[0][:, SLOTS + T :], 0.0)
-        nc.vector.memset(w2s[:].bitcast(I32), 0)
         for b in range(1, ROW_BLOCKS):
             nc.scalar.activation(ys[b][:, SLOTS + T :], ys[0][:, SLOTS + T :], RELU)
         make_identity(nc, ident[:])
 
-        def load_scale_rows(plane, scales, q):
+        def load_scale_rows(plane, scales, experts, q):
             nc.sync.dma_start(
-                plane[32 * q : 32 * q + 4, :, :].bitcast(I32),
-                scales[:, 0, 4 * q : 4 * q + 4, :].rearrange("e r n -> r e n").bitcast(I32),
+                plane[32 * q : 32 * q + 4, experts, :].bitcast(I32),
+                scales[experts, 0, 4 * q : 4 * q + 4, :].rearrange("e r n -> r e n").bitcast(I32),
             )
 
         def load_words(tile, words, experts, cols):
@@ -76,23 +78,26 @@ def tile_moe_cpy_mlp_relu_kernel(
             )
 
         everything = slice(0, 2 * H)
-        nc.sync.dma_start(slot_list[:], offs)
         nc.sync.dma_start(xw[:].bitcast(I32), x_words[0].rearrange("p t d -> p (t d)").bitcast(I32))
         for q in range(4):
             rows = x_scales[0, 4 * q : 4 * q + 4, :].bitcast(I32)
             nc.sync.dma_start(xs[32 * q : 32 * (q + 1), :].bitcast(I32), rows.unsqueeze(0).to_broadcast([8, 4, T // 4]))
+        nc.sync.dma_start(slot_list[:], offs)
         load_words(w1w, w1_words, slice(0, 1), everything)
-        load_words(w1w, w1_words, slice(1, 2), everything)
         for q in range(4):
-            load_scale_rows(w1s, w1_scales, q)
+            load_scale_rows(w1s, w1_scales, slice(0, EARLY), q)
+        load_words(w1w, w1_words, slice(1, 2), everything)
+        for r, pos in enumerate((pos1, pos2, pos3, pos4)):
+            nc.sync.dma_start(pos_lists[r][:], pos)
+        for q in range(4):
+            load_scale_rows(w1s, w1_scales, slice(EARLY, E), q)
         load_words(w1w, w1_words, slice(2, 4), everything)
         for q in range(4):
-            load_scale_rows(w2s, w2_scales, q)
+            load_scale_rows(w2s, w2_scales, slice(0, E), q)
         load_words(w2w, w2_words, slice(0, E), slice(0, 2 * P))
         load_words(w1w, w1_words, slice(4, E), everything)
         nc.sync.dma_start(ys[0][:, SLOTS : SLOTS + T], xr[0:P, :])
-        for r, pos in enumerate((pos1, pos2, pos3, pos4)):
-            nc.sync.dma_start(pos_lists[r][:], pos)
+        for r in range(TOP):
             nc.sync.dma_start(gates[:, r, :], gate[r])
         load_words(w2w, w2_words, slice(0, E), slice(2 * P, 2 * K))
         for b in range(1, ROW_BLOCKS):
@@ -120,14 +125,14 @@ def tile_moe_cpy_mlp_relu_kernel(
             hb = ring.tile([P, H], BF16, name="hb", align_bytes=64, bufs=4)
             dst = hb[:].rearrange("p (u m d) -> p u m d", u=2, d=2)
             src = acc[:].rearrange("p (m u d) -> p u m d", u=2, d=2)
-            if g == LAST_TILE:
+            if g in H_ON_VECTOR:
                 nc.vector.tensor_scalar_max(dst, src, 0.0)
             else:
                 nc.scalar.activation(dst, src, RELU)
             return hb
 
         def turn_and_quantise(e, pair):
-            ht = ring.tile([P, 4 * C], BF16, name="ht", align_bytes=64)
+            ht = ring.tile([P, 4 * C], BF16, name="ht", align_bytes=64, bufs=E)
             split = e == E - 1
             for s, hb in enumerate(pair):
                 bank = wide[0] if split and s == 0 else turn[e % 2]
@@ -167,34 +172,49 @@ def tile_moe_cpy_mlp_relu_kernel(
             if e >= E - 2:
                 second_layer(0, [e], back[(e + 1) % 2], nc.vector.tensor_copy)
 
-        for b in range(ROW_BLOCKS):
-            last = b == ROW_BLOCKS - 1
-            if not last:
-                for pair in range(E // 2):
-                    second_layer(b + 1, [2 * pair, 2 * pair + 1], wide[(pair + 1) % 4], nc.scalar.copy)
-            products = []
-            for r in range(TOP):
-                prod = ring.tile([P, T], F32, name="prod", align_bytes=64, bufs=2 * TOP)
-                nc.vector.tensor_tensor(prod[:], ys[b][:].indirect(pos_lists[r][:]), gates[:, r, :], MULT)
-                products.append(prod)
-            summed = products[:-1] if last else products
+        def turned_sum(dst, products, tok, first, final):
+            for r, prod in products:
+                nc.tensor.matmul(
+                    dst, lhsT=prod[:, tok : tok + P], rhs=ident[:],
+                    start=(r == first), stop=(r == final), is_transpose=True,
+                )
+
+        def weighted(b, r):
+            prod = ring.tile([P, T], F32, name="prod", align_bytes=64, bufs=2 * TOP)
+            nc.vector.tensor_tensor(prod[:], ys[b][:].indirect(pos_lists[r][:]), gates[:, r, :], MULT)
+            return prod
+
+        def turn_back(half, total_sb):
+            for j in range(HALF // P):
+                nc.tensor.transpose(back[half][:, j * P : (j + 1) * P], total_sb[:, j * P : (j + 1) * P], ident[:])
+
+        for b in range(ROW_BLOCKS - 1):
+            for pair in range(E // 2):
+                second_layer(b + 1, [2 * pair, 2 * pair + 1], wide[(pair + 1) % 4], nc.scalar.copy)
+            products = [(r, weighted(b, r)) for r in range(TOP)]
             for half in range(2):
-                total = turn[half]
                 for j in range(HALF // P):
-                    tok = half * HALF + j * P
-                    for r, prod in enumerate(summed):
-                        nc.tensor.matmul(
-                            total[:, j * P : (j + 1) * P], lhsT=prod[:, tok : tok + P], rhs=ident[:],
-                            start=(r == 0), stop=(r == len(summed) - 1), is_transpose=True,
-                        )
+                    turned_sum(turn[half][:, j * P : (j + 1) * P], products, half * HALF + j * P, 0, TOP - 1)
                 total_sb = ring.tile([P, HALF], F32, name="total_sb", align_bytes=64)
-                nc.scalar.copy(total_sb[:], total[:, :HALF])
-                for j in range(HALF // P):
-                    nc.tensor.transpose(back[half][:, j * P : (j + 1) * P], total_sb[:, j * P : (j + 1) * P], ident[:])
+                nc.scalar.copy(total_sb[:], turn[half][:, :HALF])
+                turn_back(half, total_sb)
                 result = ring.tile([P, HALF], F32, name="result", align_bytes=64)
-                toks = slice(half * HALF, (half + 1) * HALF)
-                if last:
-                    nc.vector.tensor_tensor(result[:], back[half][:, :HALF], products[-1][:, toks], ADD)
-                else:
-                    nc.scalar.copy(result[:], back[half][:, :HALF])
-                nc.sync.dma_start(out[b * P : (b + 1) * P, toks], result[:])
+                nc.scalar.copy(result[:], back[half][:, :HALF])
+                nc.sync.dma_start(out[b * P : (b + 1) * P, half * HALF : (half + 1) * HALF], result[:])
+
+        b = ROW_BLOCKS - 1
+        open_banks = wide + turn
+        for r in range(TOP - 1):
+            prod = weighted(b, r)
+            for j, bank in enumerate(open_banks):
+                turned_sum(bank[:, :P], [(r, prod)], j * P, 0, TOP - 2)
+        prod = weighted(b, TOP - 1)
+        for half in range(2):
+            total_sb = ring.tile([P, HALF], F32, name="total_sb", align_bytes=64)
+            for j in range(HALF // P):
+                nc.scalar.copy(total_sb[:, j * P : (j + 1) * P], open_banks[half * (HALF // P) + j][:, :P])
+            turn_back(half, total_sb)
+            result = ring.tile([P, HALF], F32, name="result", align_bytes=64)
+            toks = slice(half * HALF, (half + 1) * HALF)
+            nc.vector.tensor_tensor(result[:], back[half][:, :HALF], prod[:, toks], ADD)
+            nc.sync.dma_start(out[b * P : (b + 1) * P, toks], result[:])

@@ -25,9 +25,10 @@ P = 128
 BANK = 512
 ROW_BLOCKS = K // P
 HALF = T // 2
-GATHER_CUTS = [0, 256, 512, 768, 1024, 1536, 2048]
+GATHER_CUTS = [0, 256, 512, 1024, 1536, 2048]
 EARLY = 2
-H_ON_VECTOR = {13, 15}
+H_ON_VECTOR = {11, 13, 15}
+WIDE = 6
 
 
 def tile_moe_cpy_mlp_relu_kernel(
@@ -46,29 +47,31 @@ def tile_moe_cpy_mlp_relu_kernel(
         w1w = keep.tile([P, E, 2 * H], U8, name="w1w", align_bytes=64)
         w2w = keep.tile([P, E, 2 * K], U8, name="w2w", align_bytes=64)
         w1s = keep.tile([P, E, H], U8, name="w1s", align_bytes=64)
-        w2s = keep.tile([P, E, K], U8, name="w2s", align_bytes=64)
+        w2s_first = keep.tile([P, E, P], U8, name="w2s_first", align_bytes=64)
+        w2s_rest = keep.tile([P, E, K - P], U8, name="w2s_rest", align_bytes=64)
         gates = keep.tile([P, TOP, T], F32, name="gates")
         ys = [keep.tile([P, COLS], F32, name="y%d" % b, align_bytes=64) for b in range(ROW_BLOCKS)]
         ident = keep.tile([P, P], F32, name="ident", align_bytes=64)
         hq = keep.tile([P, SLOTS], U32, name="hq", align_bytes=64)
         hs = keep.tile([P, SLOTS], U8, name="hs", align_bytes=64)
 
-        wide = [psum.tile([P, BANK], F32, name="wide%d" % i) for i in range(4)]
+        wide = [psum.tile([P, BANK], F32, name="wide%d" % i) for i in range(WIDE)]
         turn = [psum.tile([P, BANK], F32, name="turn%d" % i) for i in range(2)]
-        back = [psum.tile([P, BANK], F32, name="back%d" % i) for i in range(2)]
+        back = wide[1:3]
 
         nc.vector.memset(w1s[:, :EARLY, :].bitcast(I32), 0)
         nc.vector.memset(w1s[:, EARLY:, :].bitcast(I32), 0)
-        nc.gpsimd.memset(w2s[:].bitcast(I32), 0)
+        nc.vector.memset(w2s_first[:].bitcast(I32), 0)
+        nc.gpsimd.memset(w2s_rest[:].bitcast(I32), 0)
         nc.vector.memset(ys[0][:, SLOTS + T :], 0.0)
         for b in range(1, ROW_BLOCKS):
             nc.scalar.activation(ys[b][:, SLOTS + T :], ys[0][:, SLOTS + T :], RELU)
         make_identity(nc, ident[:])
 
-        def load_scale_rows(plane, scales, experts, q):
+        def load_scale_rows(plane, scales, experts, cols, q):
             nc.sync.dma_start(
                 plane[32 * q : 32 * q + 4, experts, :].bitcast(I32),
-                scales[experts, 0, 4 * q : 4 * q + 4, :].rearrange("e r n -> r e n").bitcast(I32),
+                scales[experts, 0, 4 * q : 4 * q + 4, cols].rearrange("e r n -> r e n").bitcast(I32),
             )
 
         def load_words(tile, words, experts, cols):
@@ -85,20 +88,22 @@ def tile_moe_cpy_mlp_relu_kernel(
         nc.sync.dma_start(slot_list[:], offs)
         load_words(w1w, w1_words, slice(0, 1), everything)
         for q in range(4):
-            load_scale_rows(w1s, w1_scales, slice(0, EARLY), q)
+            load_scale_rows(w1s, w1_scales, slice(0, EARLY), slice(0, H), q)
         load_words(w1w, w1_words, slice(1, 2), everything)
         for r, pos in enumerate((pos1, pos2, pos3, pos4)):
             nc.sync.dma_start(pos_lists[r][:], pos)
         for q in range(4):
-            load_scale_rows(w1s, w1_scales, slice(EARLY, E), q)
+            load_scale_rows(w1s, w1_scales, slice(EARLY, E), slice(0, H), q)
         load_words(w1w, w1_words, slice(2, 4), everything)
         for q in range(4):
-            load_scale_rows(w2s, w2_scales, slice(0, E), q)
+            load_scale_rows(w2s_first, w2_scales, slice(0, E), slice(0, P), q)
         load_words(w2w, w2_words, slice(0, E), slice(0, 2 * P))
         load_words(w1w, w1_words, slice(4, E), everything)
         nc.sync.dma_start(ys[0][:, SLOTS : SLOTS + T], xr[0:P, :])
         for r in range(TOP):
             nc.sync.dma_start(gates[:, r, :], gate[r])
+        for q in range(4):
+            load_scale_rows(w2s_rest, w2_scales, slice(0, E), slice(P, K), q)
         load_words(w2w, w2_words, slice(0, E), slice(2 * P, 2 * K))
         for b in range(1, ROW_BLOCKS):
             nc.sync.dma_start(ys[b][:, SLOTS : SLOTS + T], xr[b * P : (b + 1) * P, :])
@@ -117,12 +122,12 @@ def tile_moe_cpy_mlp_relu_kernel(
         def first_layer(g):
             words, scale = gathered[g]
             e = g * P // C
-            acc = wide[g % 4]
+            acc = wide[g % WIDE]
             nc.tensor.matmul_mx(
                 out=acc[:], lhsT=words.bitcast(FP8X4), lhsT_scale=scale,
                 rhs=w1w[:, e, :].bitcast(FP4X4), rhs_scale=w1s[:, e, :], start=True, stop=True,
             )
-            hb = ring.tile([P, H], BF16, name="hb", align_bytes=64, bufs=4)
+            hb = ring.tile([P, H], BF16, name="hb", align_bytes=64, bufs=E)
             dst = hb[:].rearrange("p (u m d) -> p u m d", u=2, d=2)
             src = acc[:].rearrange("p (m u d) -> p u m d", u=2, d=2)
             if g in H_ON_VECTOR:
@@ -133,20 +138,16 @@ def tile_moe_cpy_mlp_relu_kernel(
 
         def turn_and_quantise(e, pair):
             ht = ring.tile([P, 4 * C], BF16, name="ht", align_bytes=64, bufs=E)
-            split = e == E - 1
+            bank = turn[e % 2]
             for s, hb in enumerate(pair):
-                bank = wide[0] if split and s == 0 else turn[e % 2]
                 words = hb[:].bitcast(F32)
                 for u in range(2):
                     col = (2 * s + u) * P
                     nc.tensor.transpose(bank[:, col : col + P], words[:, u * P : (u + 1) * P], ident[:])
-            dst = ht[:].bitcast(F32).rearrange("p (s c u) -> p s c u", s=2, u=2)
-            src = turn[e % 2][:].rearrange("p (s u c) -> p s c u", s=2, u=2)
-            if split:
-                nc.scalar.copy(dst[:, 0], wide[0][:].rearrange("p (s u c) -> p s c u", s=2, u=2)[:, 0])
-                nc.vector.tensor_copy(dst[:, 1], src[:, 1])
-            else:
-                nc.scalar.copy(dst, src)
+            nc.scalar.copy(
+                ht[:].bitcast(F32).rearrange("p (s c u) -> p s c u", s=2, u=2),
+                bank[:].rearrange("p (s u c) -> p s c u", s=2, u=2),
+            )
             cols = slice(e * C, (e + 1) * C)
             nc.vector.quantize_mx(out=hq[:, cols].bitcast(FP8X4), scales=hs[:, cols], in_=ht[:])
 
@@ -155,7 +156,8 @@ def tile_moe_cpy_mlp_relu_kernel(
                 cols = slice(e * C, (e + 1) * C)
                 nc.tensor.matmul_mx(
                     out=bank[:, j * C : (j + 1) * C],
-                    lhsT=w2w[:, e, 2 * P * b : 2 * P * (b + 1)].bitcast(FP4X4), lhsT_scale=w2s[:, e, P * b : P * (b + 1)],
+                    lhsT=w2w[:, e, 2 * P * b : 2 * P * (b + 1)].bitcast(FP4X4),
+                    lhsT_scale=w2s_rest[:, e, P * (b - 1) : P * b] if b else w2s_first[:, e, :],
                     rhs=hq[:, cols].bitcast(FP8X4), rhs_scale=hs[:, cols], start=True, stop=True,
                 )
             copy(ys[b][:, experts[0] * C : (experts[-1] + 1) * C], bank[:, : len(experts) * C])
@@ -163,14 +165,12 @@ def tile_moe_cpy_mlp_relu_kernel(
         for e in range(E):
             if e * C in GATHER_CUTS:
                 gather_tokens(e * C, GATHER_CUTS[GATHER_CUTS.index(e * C) + 1])
-            pair = [first_layer(2 * e), first_layer(2 * e + 1)]
-            if e == E - 2:
-                second_layer(0, [0, 1], back[0], nc.vector.tensor_copy)
-                second_layer(0, [2, 3], back[1], nc.vector.tensor_copy)
-                second_layer(0, [4, 5], back[0], nc.vector.tensor_copy)
-            turn_and_quantise(e, pair)
-            if e >= E - 2:
-                second_layer(0, [e], back[(e + 1) % 2], nc.vector.tensor_copy)
+            turn_and_quantise(e, [first_layer(2 * e), first_layer(2 * e + 1)])
+        second_layer(0, [7], wide[0], nc.vector.tensor_copy)
+        second_layer(0, [0, 1], wide[4], nc.vector.tensor_copy)
+        second_layer(0, [2, 3], turn[0], nc.scalar.copy)
+        second_layer(0, [4, 5], turn[1], nc.scalar.copy)
+        second_layer(0, [6], wide[5], nc.scalar.copy)
 
         def turned_sum(dst, products, tok, first, final):
             for r, prod in products:
@@ -188,9 +188,10 @@ def tile_moe_cpy_mlp_relu_kernel(
             for j in range(HALF // P):
                 nc.tensor.transpose(back[half][:, j * P : (j + 1) * P], total_sb[:, j * P : (j + 1) * P], ident[:])
 
+        later = [wide[5], wide[0]]
         for b in range(ROW_BLOCKS - 1):
             for pair in range(E // 2):
-                second_layer(b + 1, [2 * pair, 2 * pair + 1], wide[(pair + 1) % 4], nc.scalar.copy)
+                second_layer(b + 1, [2 * pair, 2 * pair + 1], (later if b else turn)[pair % 2], nc.scalar.copy)
             products = [(r, weighted(b, r)) for r in range(TOP)]
             for half in range(2):
                 for j in range(HALF // P):
@@ -203,7 +204,7 @@ def tile_moe_cpy_mlp_relu_kernel(
                 nc.sync.dma_start(out[b * P : (b + 1) * P, half * HALF : (half + 1) * HALF], result[:])
 
         b = ROW_BLOCKS - 1
-        open_banks = wide + turn
+        open_banks = [wide[0]] + wide[3:] + turn
         for r in range(TOP - 1):
             prod = weighted(b, r)
             for j, bank in enumerate(open_banks):

@@ -167,55 +167,40 @@ def tile_moe_cpy_mlp_relu_kernel(
                 gather_tokens(e * C, GATHER_CUTS[GATHER_CUTS.index(e * C) + 1])
             turn_and_quantise(e, [first_layer(2 * e), first_layer(2 * e + 1)])
         second_layer(0, [7], wide[0], nc.vector.tensor_copy)
-        second_layer(0, [0, 1], wide[4], nc.vector.tensor_copy)
-        second_layer(0, [2, 3], turn[0], nc.scalar.copy)
+        second_layer(0, [0, 1], wide[4], nc.scalar.copy)
+        second_layer(0, [2, 3], turn[0], nc.vector.tensor_copy)
         second_layer(0, [4, 5], turn[1], nc.scalar.copy)
         second_layer(0, [6], wide[5], nc.scalar.copy)
 
-        def turned_sum(dst, products, tok, first, final):
-            for r, prod in products:
-                nc.tensor.matmul(
-                    dst, lhsT=prod[:, tok : tok + P], rhs=ident[:],
-                    start=(r == first), stop=(r == final), is_transpose=True,
-                )
+        sums = turn + [wide[5], wide[4], wide[3], wide[0]]
+        jobs = [(1, 0), (1, 1), (1, 2), (1, 3), (2, 3), (2, 0), (2, 1), (2, 2), (3, 0), (3, 1), (3, 2), (3, 3)]
+        for i, (b, pair) in enumerate(jobs):
+            second_layer(b, [2 * pair, 2 * pair + 1], sums[i % len(sums)], nc.scalar.copy)
 
-        def weighted(b, r):
-            prod = ring.tile([P, T], F32, name="prod", align_bytes=64, bufs=2 * TOP)
-            nc.vector.tensor_tensor(prod[:], ys[b][:].indirect(pos_lists[r][:]), gates[:, r, :], MULT)
-            return prod
-
-        def turn_back(half, total_sb):
-            for j in range(HALF // P):
-                nc.tensor.transpose(back[half][:, j * P : (j + 1) * P], total_sb[:, j * P : (j + 1) * P], ident[:])
-
-        later = [wide[5], wide[0]]
-        for b in range(ROW_BLOCKS - 1):
-            for pair in range(E // 2):
-                second_layer(b + 1, [2 * pair, 2 * pair + 1], (later if b else turn)[pair % 2], nc.scalar.copy)
-            products = [(r, weighted(b, r)) for r in range(TOP)]
+        for b in range(ROW_BLOCKS):
+            last = b == ROW_BLOCKS - 1
+            turned = TOP - 1 if last else TOP
+            for r in range(TOP):
+                prod = ring.tile([P, T], F32, name="prod", align_bytes=64, bufs=2 * TOP)
+                nc.vector.tensor_tensor(prod[:], ys[b][:].indirect(pos_lists[r][:]), gates[:, r, :], MULT)
+                if r < turned:
+                    for j, bank in enumerate(sums):
+                        nc.tensor.matmul(
+                            bank[:, :P], lhsT=prod[:, j * P : (j + 1) * P], rhs=ident[:],
+                            start=(r == 0), stop=(r == turned - 1), is_transpose=True,
+                        )
             for half in range(2):
+                total = ring.tile([P, HALF], F32, name="total", align_bytes=64)
                 for j in range(HALF // P):
-                    turned_sum(turn[half][:, j * P : (j + 1) * P], products, half * HALF + j * P, 0, TOP - 1)
-                total_sb = ring.tile([P, HALF], F32, name="total_sb", align_bytes=64)
-                nc.scalar.copy(total_sb[:], turn[half][:, :HALF])
-                turn_back(half, total_sb)
+                    cols = slice(j * P, (j + 1) * P)
+                    nc.scalar.copy(total[:, cols], sums[half * (HALF // P) + j][:, :P])
+                    nc.tensor.transpose(back[half][:, cols], total[:, cols], ident[:])
                 result = ring.tile([P, HALF], F32, name="result", align_bytes=64)
-                nc.scalar.copy(result[:], back[half][:, :HALF])
-                nc.sync.dma_start(out[b * P : (b + 1) * P, half * HALF : (half + 1) * HALF], result[:])
-
-        b = ROW_BLOCKS - 1
-        open_banks = [wide[0]] + wide[3:] + turn
-        for r in range(TOP - 1):
-            prod = weighted(b, r)
-            for j, bank in enumerate(open_banks):
-                turned_sum(bank[:, :P], [(r, prod)], j * P, 0, TOP - 2)
-        prod = weighted(b, TOP - 1)
-        for half in range(2):
-            total_sb = ring.tile([P, HALF], F32, name="total_sb", align_bytes=64)
-            for j in range(HALF // P):
-                nc.scalar.copy(total_sb[:, j * P : (j + 1) * P], open_banks[half * (HALF // P) + j][:, :P])
-            turn_back(half, total_sb)
-            result = ring.tile([P, HALF], F32, name="result", align_bytes=64)
-            toks = slice(half * HALF, (half + 1) * HALF)
-            nc.vector.tensor_tensor(result[:], back[half][:, :HALF], prod[:, toks], ADD)
-            nc.sync.dma_start(out[b * P : (b + 1) * P, toks], result[:])
+                cuts = [0, HALF - P, HALF] if last and half == 1 else [0, HALF]
+                for lo, hi in zip(cuts, cuts[1:]):
+                    toks = slice(half * HALF + lo, half * HALF + hi)
+                    if last:
+                        nc.vector.tensor_tensor(result[:, lo:hi], back[half][:, lo:hi], prod[:, toks], ADD)
+                    else:
+                        nc.scalar.copy(result[:, lo:hi], back[half][:, lo:hi])
+                    nc.sync.dma_start(out[b * P : (b + 1) * P, toks], result[:, lo:hi])

@@ -23,12 +23,15 @@ ADD = mybir.AluOpType.add
 
 P = 128
 BANK = 512
+QUADRANTS = 4
 ROW_BLOCKS = K // P
 HALF = T // 2
+FP4_BYTES = 2
+
 GATHER_CUTS = [0, 256, 512, 1024, 1536, 2048]
-EARLY = 2
-H_ON_VECTOR = {11, 13, 15}
-WIDE = 6
+SCALE_GROUPS = [slice(0, 2), slice(2, 4), slice(4, E)]
+RELU_ON_VECTOR = {11, 13, 15}
+LAYER1_BANKS = 6
 
 
 def tile_moe_cpy_mlp_relu_kernel(
@@ -44,75 +47,62 @@ def tile_moe_cpy_mlp_relu_kernel(
         pos_lists = [keep.tile([P, T // 16], U16, name="pos_list%d" % r) for r in range(TOP)]
         xw = keep.tile([P, T], U32, name="xw", align_bytes=64)
         xs = keep.tile([P, T], U8, name="xs", align_bytes=64)
-        w1w = keep.tile([P, E, 2 * H], U8, name="w1w", align_bytes=64)
-        w2w = keep.tile([P, E, 2 * K], U8, name="w2w", align_bytes=64)
+        w1w = keep.tile([P, E, FP4_BYTES * H], U8, name="w1w", align_bytes=64)
         w1s = keep.tile([P, E, H], U8, name="w1s", align_bytes=64)
+        w2w_first = keep.tile([P, E, FP4_BYTES * P], U8, name="w2w_first", align_bytes=64)
         w2s_first = keep.tile([P, E, P], U8, name="w2s_first", align_bytes=64)
         w2s_rest = keep.tile([P, E, K - P], U8, name="w2s_rest", align_bytes=64)
-        gates = keep.tile([P, TOP, T], F32, name="gates")
-        ys = [keep.tile([P, COLS], F32, name="y%d" % b, align_bytes=64) for b in range(ROW_BLOCKS)]
         ident = keep.tile([P, P], F32, name="ident", align_bytes=64)
         hq = keep.tile([P, SLOTS], U32, name="hq", align_bytes=64)
         hs = keep.tile([P, SLOTS], U8, name="hs", align_bytes=64)
 
-        wide = [psum.tile([P, BANK], F32, name="wide%d" % i) for i in range(WIDE)]
+        wide = [psum.tile([P, BANK], F32, name="wide%d" % i) for i in range(LAYER1_BANKS)]
         turn = [psum.tile([P, BANK], F32, name="turn%d" % i) for i in range(2)]
-        back = wide[1:3]
 
-        nc.vector.memset(w1s[:, :EARLY, :].bitcast(I32), 0)
-        nc.vector.memset(w1s[:, EARLY:, :].bitcast(I32), 0)
+        for experts in SCALE_GROUPS:
+            nc.vector.memset(w1s[:, experts, :].bitcast(I32), 0)
         nc.vector.memset(w2s_first[:].bitcast(I32), 0)
         nc.gpsimd.memset(w2s_rest[:].bitcast(I32), 0)
-        nc.vector.memset(ys[0][:, SLOTS + T :], 0.0)
-        for b in range(1, ROW_BLOCKS):
-            nc.scalar.activation(ys[b][:, SLOTS + T :], ys[0][:, SLOTS + T :], RELU)
         make_identity(nc, ident[:])
 
-        def load_scale_rows(plane, scales, experts, cols, q):
+        def load_scale_rows(dst, scales, experts, cols):
+            for q in range(QUADRANTS):
+                nc.sync.dma_start(
+                    dst[32 * q : 32 * q + 4, :, :].bitcast(I32),
+                    scales[experts, 0, 4 * q : 4 * q + 4, cols].rearrange("e r n -> r e n").bitcast(I32),
+                )
+
+        def load_words(dst, words, experts, byte_cols):
             nc.sync.dma_start(
-                plane[32 * q : 32 * q + 4, experts, :].bitcast(I32),
-                scales[experts, 0, 4 * q : 4 * q + 4, cols].rearrange("e r n -> r e n").bitcast(I32),
+                dst.bitcast(I32), words[experts, 0, :, byte_cols].rearrange("e p n -> p e n").bitcast(I32)
             )
 
-        def load_words(tile, words, experts, cols):
-            nc.sync.dma_start(
-                tile[:, experts, cols].bitcast(I32),
-                words[experts, 0, :, cols].rearrange("e p n -> p e n").bitcast(I32),
-            )
+        def load_w1_words(experts):
+            load_words(w1w[:, experts, :], w1_words, experts, slice(0, FP4_BYTES * H))
 
-        everything = slice(0, 2 * H)
         nc.sync.dma_start(xw[:].bitcast(I32), x_words[0].rearrange("p t d -> p (t d)").bitcast(I32))
-        for q in range(4):
+        for q in range(QUADRANTS):
             rows = x_scales[0, 4 * q : 4 * q + 4, :].bitcast(I32)
             nc.sync.dma_start(xs[32 * q : 32 * (q + 1), :].bitcast(I32), rows.unsqueeze(0).to_broadcast([8, 4, T // 4]))
         nc.sync.dma_start(slot_list[:], offs)
-        load_words(w1w, w1_words, slice(0, 1), everything)
-        for q in range(4):
-            load_scale_rows(w1s, w1_scales, slice(0, EARLY), slice(0, H), q)
-        load_words(w1w, w1_words, slice(1, 2), everything)
+
+        all_experts = slice(0, E)
+        load_w1_words(slice(0, 1))
+        for experts, next_words in zip(SCALE_GROUPS, (slice(1, 2), slice(2, 4), slice(4, 6))):
+            load_scale_rows(w1s[:, experts, :], w1_scales, experts, slice(0, H))
+            load_w1_words(next_words)
+        load_scale_rows(w2s_first[:], w2_scales, all_experts, slice(0, P))
+        load_w1_words(slice(6, E))
+        load_words(w2w_first[:], w2_words, all_experts, slice(0, FP4_BYTES * P))
         for r, pos in enumerate((pos1, pos2, pos3, pos4)):
             nc.sync.dma_start(pos_lists[r][:], pos)
-        for q in range(4):
-            load_scale_rows(w1s, w1_scales, slice(EARLY, E), slice(0, H), q)
-        load_words(w1w, w1_words, slice(2, 4), everything)
-        for q in range(4):
-            load_scale_rows(w2s_first, w2_scales, slice(0, E), slice(0, P), q)
-        load_words(w2w, w2_words, slice(0, E), slice(0, 2 * P))
-        load_words(w1w, w1_words, slice(4, E), everything)
-        nc.sync.dma_start(ys[0][:, SLOTS : SLOTS + T], xr[0:P, :])
-        for r in range(TOP):
-            nc.sync.dma_start(gates[:, r, :], gate[r])
-        for q in range(4):
-            load_scale_rows(w2s_rest, w2_scales, slice(0, E), slice(P, K), q)
-        load_words(w2w, w2_words, slice(0, E), slice(2 * P, 2 * K))
-        for b in range(1, ROW_BLOCKS):
-            nc.sync.dma_start(ys[b][:, SLOTS : SLOTS + T], xr[b * P : (b + 1) * P, :])
+        load_scale_rows(w2s_rest[:], w2_scales, all_experts, slice(P, K))
 
         gathered = {}
 
         def gather_tokens(lo, hi):
-            words = keep.tile([P, hi - lo], U32, name="xg%d" % lo, align_bytes=64)
-            scale = keep.tile([P, hi - lo], U8, name="sg%d" % lo, align_bytes=64)
+            words = keep.tile([P, hi - lo], U32, name="xg%d" % lo, tag="words%d" % lo, align_bytes=64)
+            scale = keep.tile([P, hi - lo], U8, name="sg%d" % lo, tag="bytes%d" % lo, align_bytes=64)
             cut = slot_list[:, lo // 16 : hi // 16]
             nc.vector.tensor_copy(words[:], xw[:].indirect(cut))
             nc.vector.tensor_copy(scale[:], xs[:].indirect(cut))
@@ -122,7 +112,7 @@ def tile_moe_cpy_mlp_relu_kernel(
         def first_layer(g):
             words, scale = gathered[g]
             e = g * P // C
-            acc = wide[g % WIDE]
+            acc = wide[g % LAYER1_BANKS]
             nc.tensor.matmul_mx(
                 out=acc[:], lhsT=words.bitcast(FP8X4), lhsT_scale=scale,
                 rhs=w1w[:, e, :].bitcast(FP4X4), rhs_scale=w1s[:, e, :], start=True, stop=True,
@@ -130,20 +120,20 @@ def tile_moe_cpy_mlp_relu_kernel(
             hb = ring.tile([P, H], BF16, name="hb", align_bytes=64, bufs=E)
             dst = hb[:].rearrange("p (u m d) -> p u m d", u=2, d=2)
             src = acc[:].rearrange("p (m u d) -> p u m d", u=2, d=2)
-            if g in H_ON_VECTOR:
+            if g in RELU_ON_VECTOR:
                 nc.vector.tensor_scalar_max(dst, src, 0.0)
             else:
                 nc.scalar.activation(dst, src, RELU)
             return hb
 
-        def turn_and_quantise(e, pair):
-            ht = ring.tile([P, 4 * C], BF16, name="ht", align_bytes=64, bufs=E)
+        def turn_and_quantise(e, groups):
             bank = turn[e % 2]
-            for s, hb in enumerate(pair):
-                words = hb[:].bitcast(F32)
+            for s, hb in enumerate(groups):
+                pairs = hb[:].bitcast(F32)
                 for u in range(2):
                     col = (2 * s + u) * P
-                    nc.tensor.transpose(bank[:, col : col + P], words[:, u * P : (u + 1) * P], ident[:])
+                    nc.tensor.transpose(bank[:, col : col + P], pairs[:, u * P : (u + 1) * P], ident[:])
+            ht = ring.tile([P, 4 * C], BF16, name="ht", align_bytes=64, bufs=E)
             nc.scalar.copy(
                 ht[:].bitcast(F32).rearrange("p (s c u) -> p s c u", s=2, u=2),
                 bank[:].rearrange("p (s u c) -> p s c u", s=2, u=2),
@@ -151,31 +141,52 @@ def tile_moe_cpy_mlp_relu_kernel(
             cols = slice(e * C, (e + 1) * C)
             nc.vector.quantize_mx(out=hq[:, cols].bitcast(FP8X4), scales=hs[:, cols], in_=ht[:])
 
-        def second_layer(b, experts, bank, copy):
-            for j, e in enumerate(experts):
-                cols = slice(e * C, (e + 1) * C)
-                nc.tensor.matmul_mx(
-                    out=bank[:, j * C : (j + 1) * C],
-                    lhsT=w2w[:, e, 2 * P * b : 2 * P * (b + 1)].bitcast(FP4X4),
-                    lhsT_scale=w2s_rest[:, e, P * (b - 1) : P * b] if b else w2s_first[:, e, :],
-                    rhs=hq[:, cols].bitcast(FP8X4), rhs_scale=hs[:, cols], start=True, stop=True,
-                )
-            copy(ys[b][:, experts[0] * C : (experts[-1] + 1) * C], bank[:, : len(experts) * C])
+        def late_tile(shape, dtype, name, tag):
+            return keep.tile(shape, dtype, name=name, tag=tag, align_bytes=64)
+
+        def row_block_tile(b, tag):
+            y = late_tile([P, COLS], F32, "y%d" % b, tag)
+            nc.sync.dma_start(y[:, SLOTS : SLOTS + T], xr[b * P : (b + 1) * P, :])
+            nc.gpsimd.memset(y[:, SLOTS + T :], 0.0)
+            return y
 
         for e in range(E):
             if e * C in GATHER_CUTS:
                 gather_tokens(e * C, GATHER_CUTS[GATHER_CUTS.index(e * C) + 1])
             turn_and_quantise(e, [first_layer(2 * e), first_layer(2 * e + 1)])
+
+        first, second, third = GATHER_CUTS[:3]
+        gates = late_tile([P, TOP, T], F32, "gates", "words%d" % first)
+        for r in range(TOP):
+            nc.sync.dma_start(gates[:, r, :], gate[r])
+        w2w_rest = late_tile([P, E, FP4_BYTES * (K - P)], U8, "w2w_rest", "words%d" % third)
+        load_words(w2w_rest[:], w2_words, all_experts, slice(FP4_BYTES * P, FP4_BYTES * K))
+        y_tags = ["bytes%d" % first, "words%d" % second, "bytes%d" % second, "bytes%d" % third]
+        ys = [row_block_tile(b, tag) for b, tag in enumerate(y_tags)]
+
+        def second_layer(b, experts, bank, copy):
+            words, scales, block = (w2w_rest, w2s_rest, b - 1) if b else (w2w_first, w2s_first, 0)
+            for j, e in enumerate(experts):
+                cols = slice(e * C, (e + 1) * C)
+                nc.tensor.matmul_mx(
+                    out=bank[:, j * C : (j + 1) * C],
+                    lhsT=words[:, e, FP4_BYTES * P * block : FP4_BYTES * P * (block + 1)].bitcast(FP4X4),
+                    lhsT_scale=scales[:, e, P * block : P * (block + 1)],
+                    rhs=hq[:, cols].bitcast(FP8X4), rhs_scale=hs[:, cols], start=True, stop=True,
+                )
+            copy(ys[b][:, experts[0] * C : (experts[-1] + 1) * C], bank[:, : len(experts) * C])
+
         second_layer(0, [7], wide[0], nc.vector.tensor_copy)
         second_layer(0, [0, 1], wide[4], nc.scalar.copy)
         second_layer(0, [2, 3], turn[0], nc.vector.tensor_copy)
         second_layer(0, [4, 5], turn[1], nc.scalar.copy)
         second_layer(0, [6], wide[5], nc.scalar.copy)
 
-        sums = turn + [wide[5], wide[4], wide[3], wide[0]]
-        jobs = [(1, 0), (1, 1), (1, 2), (1, 3), (2, 3), (2, 0), (2, 1), (2, 2), (3, 0), (3, 1), (3, 2), (3, 3)]
-        for i, (b, pair) in enumerate(jobs):
-            second_layer(b, [2 * pair, 2 * pair + 1], sums[i % len(sums)], nc.scalar.copy)
+        back = wide[1:3]
+        sums = [wide[4], wide[3], wide[5], wide[0]] + turn
+        for b, banks in ((1, [turn[0], turn[1], wide[5], back[0]]), (2, [wide[0], turn[0], turn[1], back[1]])):
+            for pair, bank in enumerate(banks):
+                second_layer(b, [2 * pair, 2 * pair + 1], bank, nc.scalar.copy)
 
         for b in range(ROW_BLOCKS):
             last = b == ROW_BLOCKS - 1
@@ -204,3 +215,6 @@ def tile_moe_cpy_mlp_relu_kernel(
                     else:
                         nc.scalar.copy(result[:, lo:hi], back[half][:, lo:hi])
                     nc.sync.dma_start(out[b * P : (b + 1) * P, toks], result[:, lo:hi])
+            if b == 0:
+                for pair in range(E // 2):
+                    second_layer(ROW_BLOCKS - 1, [2 * pair, 2 * pair + 1], back[pair % 2], nc.scalar.copy)

from contextlib import ExitStack

import concourse.mybir as mybir
from concourse.masks import make_identity

K, T, E, C, H, TOP = 512, 768, 8, 256, 512, 4
SLOTS = E * C
PAD = 64
COLS = SLOTS + T + PAD
FLOPS = 2 * SLOTS * (K * H + H * K)

F32 = mybir.dt.float32
BF16 = mybir.dt.bfloat16
I32 = mybir.dt.int32
U32 = mybir.dt.uint32
U16 = mybir.dt.uint16
U8 = mybir.dt.uint8
FP8X4 = mybir.dt.float8_e4m3fn_x4
FP4X4 = mybir.dt.float4_e2m1fn_x4
RELU = mybir.ActivationFunctionType.Relu
MULT = mybir.AluOpType.mult
ADD = mybir.AluOpType.add

P = 128
BANK = 512
QUADRANTS = 4
ROW_BLOCKS = K // P
HALF = T // 2
FP4_BYTES = 2

GATHER_CUTS = [0, 256, 512, 1024, 1536, 2048]
SCALE_GROUPS = [slice(0, 2), slice(2, 4), slice(4, E)]
RELU_ON_VECTOR = {11, 13, 15}
LAYER1_BANKS = 6


def tile_moe_cpy_mlp_relu_kernel(
    tc, x_words, x_scales, xr, w1_words, w1_scales, w2_words, w2_scales, gate, offs, pos1, pos2, pos3, pos4, out
):
    nc = tc.nc
    with ExitStack() as ctx:
        keep = ctx.enter_context(tc.tile_pool(name="keep", bufs=1))
        ring = ctx.enter_context(tc.tile_pool(name="ring", bufs=3))
        psum = ctx.enter_context(tc.psum_pool(name="psum", bufs=1))

        slot_list = keep.tile([P, SLOTS // 16], U16, name="slot_list")
        pos_lists = [keep.tile([P, T // 16], U16, name="pos_list%d" % r) for r in range(TOP)]
        xw = keep.tile([P, T], U32, name="xw", align_bytes=64)
        xs = keep.tile([P, T], U8, name="xs", align_bytes=64)
        w1w = keep.tile([P, E, FP4_BYTES * H], U8, name="w1w", align_bytes=64)
        w1s = keep.tile([P, E, H], U8, name="w1s", align_bytes=64)
        w2w_first = keep.tile([P, E, FP4_BYTES * P], U8, name="w2w_first", align_bytes=64)
        w2s_first = keep.tile([P, E, P], U8, name="w2s_first", align_bytes=64)
        w2s_rest = keep.tile([P, E, K - P], U8, name="w2s_rest", align_bytes=64)
        ident = keep.tile([P, P], F32, name="ident", align_bytes=64)
        hq = keep.tile([P, SLOTS], U32, name="hq", align_bytes=64)
        hs = keep.tile([P, SLOTS], U8, name="hs", align_bytes=64)

        wide = [psum.tile([P, BANK], F32, name="wide%d" % i) for i in range(LAYER1_BANKS)]
        turn = [psum.tile([P, BANK], F32, name="turn%d" % i) for i in range(2)]

        for experts in SCALE_GROUPS:
            nc.vector.memset(w1s[:, experts, :].bitcast(I32), 0)
        nc.vector.memset(w2s_first[:].bitcast(I32), 0)
        nc.gpsimd.memset(w2s_rest[:].bitcast(I32), 0)
        make_identity(nc, ident[:])

        def load_scale_rows(dst, scales, experts, cols):
            for q in range(QUADRANTS):
                nc.sync.dma_start(
                    dst[32 * q : 32 * q + 4, :, :].bitcast(I32),
                    scales[experts, 0, 4 * q : 4 * q + 4, cols].rearrange("e r n -> r e n").bitcast(I32),
                )

        def load_words(dst, words, experts, byte_cols):
            nc.sync.dma_start(
                dst.bitcast(I32), words[experts, 0, :, byte_cols].rearrange("e p n -> p e n").bitcast(I32)
            )

        def load_w1_words(experts):
            load_words(w1w[:, experts, :], w1_words, experts, slice(0, FP4_BYTES * H))

        nc.sync.dma_start(xw[:].bitcast(I32), x_words[0].rearrange("p t d -> p (t d)").bitcast(I32))
        for q in range(QUADRANTS):
            rows = x_scales[0, 4 * q : 4 * q + 4, :].bitcast(I32)
            nc.sync.dma_start(xs[32 * q : 32 * (q + 1), :].bitcast(I32), rows.unsqueeze(0).to_broadcast([8, 4, T // 4]))
        nc.sync.dma_start(slot_list[:], offs)

        all_experts = slice(0, E)
        load_w1_words(slice(0, 1))
        for experts, next_words in zip(SCALE_GROUPS, (slice(1, 2), slice(2, 4), slice(4, 6))):
            load_scale_rows(w1s[:, experts, :], w1_scales, experts, slice(0, H))
            load_w1_words(next_words)
        load_scale_rows(w2s_first[:], w2_scales, all_experts, slice(0, P))
        load_w1_words(slice(6, E))
        load_words(w2w_first[:], w2_words, all_experts, slice(0, FP4_BYTES * P))
        for r, pos in enumerate((pos1, pos2, pos3, pos4)):
            nc.sync.dma_start(pos_lists[r][:], pos)
        load_scale_rows(w2s_rest[:], w2_scales, all_experts, slice(P, K))

        gathered = {}

        def gather_tokens(lo, hi):
            words = keep.tile([P, hi - lo], U32, name="xg%d" % lo, tag="words%d" % lo, align_bytes=64)
            scale = keep.tile([P, hi - lo], U8, name="sg%d" % lo, tag="bytes%d" % lo, align_bytes=64)
            cut = slot_list[:, lo // 16 : hi // 16]
            nc.vector.tensor_copy(words[:], xw[:].indirect(cut))
            nc.vector.tensor_copy(scale[:], xs[:].indirect(cut))
            for s in range(lo, hi, P):
                gathered[s // P] = (words[:, s - lo : s - lo + P], scale[:, s - lo : s - lo + P])

        def first_layer(g):
            words, scale = gathered[g]
            e = g * P // C
            acc = wide[g % LAYER1_BANKS]
            nc.tensor.matmul_mx(
                out=acc[:], lhsT=words.bitcast(FP8X4), lhsT_scale=scale,
                rhs=w1w[:, e, :].bitcast(FP4X4), rhs_scale=w1s[:, e, :], start=True, stop=True,
            )
            hb = ring.tile([P, H], BF16, name="hb", align_bytes=64, bufs=E)
            dst = hb[:].rearrange("p (u m d) -> p u m d", u=2, d=2)
            src = acc[:].rearrange("p (m u d) -> p u m d", u=2, d=2)
            if g in RELU_ON_VECTOR:
                nc.vector.tensor_scalar_max(dst, src, 0.0)
            else:
                nc.scalar.activation(dst, src, RELU)
            return hb

        def turn_and_quantise(e, groups):
            bank = turn[e % 2]
            for s, hb in enumerate(groups):
                pairs = hb[:].bitcast(F32)
                for u in range(2):
                    col = (2 * s + u) * P
                    nc.tensor.transpose(bank[:, col : col + P], pairs[:, u * P : (u + 1) * P], ident[:])
            ht = ring.tile([P, 4 * C], BF16, name="ht", align_bytes=64, bufs=E)
            nc.scalar.copy(
                ht[:].bitcast(F32).rearrange("p (s c u) -> p s c u", s=2, u=2),
                bank[:].rearrange("p (s u c) -> p s c u", s=2, u=2),
            )
            cols = slice(e * C, (e + 1) * C)
            nc.vector.quantize_mx(out=hq[:, cols].bitcast(FP8X4), scales=hs[:, cols], in_=ht[:])

        def late_tile(shape, dtype, name, tag):
            return keep.tile(shape, dtype, name=name, tag=tag, align_bytes=64)

        def row_block_tile(b, tag):
            y = late_tile([P, COLS], F32, "y%d" % b, tag)
            nc.sync.dma_start(y[:, SLOTS : SLOTS + T], xr[b * P : (b + 1) * P, :])
            nc.gpsimd.memset(y[:, SLOTS + T :], 0.0)
            return y

        for e in range(E):
            if e * C in GATHER_CUTS:
                gather_tokens(e * C, GATHER_CUTS[GATHER_CUTS.index(e * C) + 1])
            turn_and_quantise(e, [first_layer(2 * e), first_layer(2 * e + 1)])

        first, second, third = GATHER_CUTS[:3]
        gates = late_tile([P, TOP, T], F32, "gates", "words%d" % first)
        for r in range(TOP):
            nc.sync.dma_start(gates[:, r, :], gate[r])
        w2w_rest = late_tile([P, E, FP4_BYTES * (K - P)], U8, "w2w_rest", "words%d" % third)
        load_words(w2w_rest[:], w2_words, all_experts, slice(FP4_BYTES * P, FP4_BYTES * K))
        y_tags = ["bytes%d" % first, "words%d" % second, "bytes%d" % second, "bytes%d" % third]
        ys = [row_block_tile(b, tag) for b, tag in enumerate(y_tags)]

        def second_layer(b, experts, bank, copy):
            words, scales, block = (w2w_rest, w2s_rest, b - 1) if b else (w2w_first, w2s_first, 0)
            for j, e in enumerate(experts):
                cols = slice(e * C, (e + 1) * C)
                nc.tensor.matmul_mx(
                    out=bank[:, j * C : (j + 1) * C],
                    lhsT=words[:, e, FP4_BYTES * P * block : FP4_BYTES * P * (block + 1)].bitcast(FP4X4),
                    lhsT_scale=scales[:, e, P * block : P * (block + 1)],
                    rhs=hq[:, cols].bitcast(FP8X4), rhs_scale=hs[:, cols], start=True, stop=True,
                )
            copy(ys[b][:, experts[0] * C : (experts[-1] + 1) * C], bank[:, : len(experts) * C])

        second_layer(0, [7], wide[0], nc.vector.tensor_copy)
        second_layer(0, [0, 1], wide[4], nc.scalar.copy)
        second_layer(0, [2, 3], turn[0], nc.vector.tensor_copy)
        second_layer(0, [4, 5], turn[1], nc.scalar.copy)
        second_layer(0, [6], wide[5], nc.scalar.copy)

        back = wide[1:3]
        sums = [wide[4], wide[3], wide[5], wide[0]] + turn
        for b, banks in ((1, [turn[0], turn[1], wide[5], back[0]]), (2, [wide[0], turn[0], turn[1], back[1]])):
            for pair, bank in enumerate(banks):
                second_layer(b, [2 * pair, 2 * pair + 1], bank, nc.scalar.copy)

        for b in range(ROW_BLOCKS):
            last = b == ROW_BLOCKS - 1
            turned = TOP - 1 if last else TOP
            for r in range(TOP):
                prod = ring.tile([P, T], F32, name="prod", align_bytes=64, bufs=2 * TOP)
                nc.vector.tensor_tensor(prod[:], ys[b][:].indirect(pos_lists[r][:]), gates[:, r, :], MULT)
                if r < turned:
                    for j, bank in enumerate(sums):
                        nc.tensor.matmul(
                            bank[:, :P], lhsT=prod[:, j * P : (j + 1) * P], rhs=ident[:],
                            start=(r == 0), stop=(r == turned - 1), is_transpose=True,
                        )
            for half in range(2):
                total = ring.tile([P, HALF], F32, name="total", align_bytes=64)
                for j in range(HALF // P):
                    cols = slice(j * P, (j + 1) * P)
                    nc.scalar.copy(total[:, cols], sums[half * (HALF // P) + j][:, :P])
                    nc.tensor.transpose(back[half][:, cols], total[:, cols], ident[:])
                result = ring.tile([P, HALF], F32, name="result", align_bytes=64)
                cuts = [0, HALF - P, HALF] if last and half == 1 else [0, HALF]
                for lo, hi in zip(cuts, cuts[1:]):
                    toks = slice(half * HALF + lo, half * HALF + hi)
                    if last:
                        nc.vector.tensor_tensor(result[:, lo:hi], back[half][:, lo:hi], prod[:, toks], ADD)
                    else:
                        nc.scalar.copy(result[:, lo:hi], back[half][:, lo:hi])
                    nc.sync.dma_start(out[b * P : (b + 1) * P, toks], result[:, lo:hi])
            if b == 0:
                for pair in range(E // 2):
                    second_layer(ROW_BLOCKS - 1, [2 * pair, 2 * pair + 1], back[pair % 2], nc.scalar.copy)
